import numpy as np
import ml_dtypes


def mxq(x, axis, fmt="e4m3"):
    dtype, down = {"e4m3": (ml_dtypes.float8_e4m3fn, 7), "e5m2": (ml_dtypes.float8_e5m2, 14)}[fmt]
    v = np.moveaxis(np.asarray(x, np.float32).astype(ml_dtypes.bfloat16).astype(np.float64), axis, -1)
    blocks = v.reshape(v.shape[:-1] + (-1, 32))
    amax = np.abs(blocks).max(-1, keepdims=True)
    byte = np.maximum(np.where(amax > 0, np.frexp(amax)[1] - 1 + 127, 0) - down, 1)
    scale = np.exp2(byte - 127.0)
    codes = (blocks / scale).astype(np.float32).astype(dtype).astype(np.float64)
    return np.moveaxis((codes * scale).reshape(v.shape), -1, axis)


WIDE = False


def mx_kscale(k):
    if not WIDE:
        return np.ones(k)
    levels = np.array([10, -10, 5, -5, 0])
    if k % 512:
        return np.exp2(np.random.permutation(np.resize(levels, k // 32))).repeat(32)
    a = np.empty((k // 512, 16))
    for p in range(k // 512):
        a[p, :8] = np.random.permutation(np.resize(levels, 8))
        for g in range(8):
            far = levels[np.abs(levels - a[p, g]) >= 10]
            a[p, g + 8] = far[np.random.randint(len(far))]
    return np.exp2(a.ravel()).repeat(32)


def f64(x):
    return np.asarray(x).astype(np.float64)


def striped(idx):
    return np.tile(idx.reshape(-1, 16).T, (8, 1)).astype(np.uint16)


def unstriped(offs):
    return offs[:16].T.reshape(-1).astype(np.int64)


def pack_weight(w):
    k, n = w.shape
    w = f64(np.asarray(w, np.float32).astype(ml_dtypes.bfloat16)).reshape(k // 32, 32, n)
    amax = np.abs(w).max(1)
    byte = np.clip(np.where(amax > 0, np.frexp(amax)[1] - 1 + 127 - 7, 1), 1, 254)
    scaled = (w * np.exp2(127.0 - byte)[:, None, :]).reshape(k, n).astype(np.float32)
    words = np.ascontiguousarray(scaled.reshape(k // 512, 128, 4, n).transpose(0, 1, 3, 2)).astype(ml_dtypes.float8_e4m3fn).view(np.uint8)
    return words, np.ascontiguousarray(byte.astype(np.uint8).reshape(k // 512, 16, n))


def unpack_weight(words, scales):
    g, p, n, _ = words.shape
    vals = np.ascontiguousarray(words).view(ml_dtypes.float8_e4m3fn).astype(np.float64) * np.repeat(np.exp2(scales.astype(np.float64) - 127.0), 8, axis=1)[..., None]
    return vals.transpose(0, 1, 3, 2).reshape(g * 512, n)


def sigmoid(v):
    return 1.0 / (1.0 + np.exp(-np.maximum(v, -700.0)))


K, T, S, N, U, D = 1024, 2048, 512, 128, 512, 3
P = 2 ** 7


def setup_inputs():
    n = np.random.standard_normal
    s = mx_kscale(K)[:, None]
    packed_xT = pack_weight(n((K, T)) * s)
    return {
        "x_words": packed_xT[0],
        "x_scales": packed_xT[1],
        "w1": (n((K, N)) / np.sqrt(K) / s).astype(np.float32),
        "sign": (np.tile(np.where(np.random.uniform(size=(D, 1, U)) < 0.5, 1.0, -1.0), (1, P, 1))).astype(np.float32),
        "thr": (-np.random.uniform(0.0, 0.5, (N, 1))).astype(np.float32),
        "offs": striped(np.random.permutation(T)[:S]),
        "hash1": striped(np.random.randint(0, S, U)),
        "hash2": striped(np.random.randint(0, S, U)),
        "hash3": striped(np.random.randint(0, S, U)),
    }


def reference(x_words, x_scales, w1, sign, thr, offs, hash1, hash2, hash3):
    xq = unpack_weight(x_words, x_scales)[:, unstriped(offs)]
    y = mxq(f64(w1), 0, "e4m3").T @ xq
    g0 = y[:, unstriped(hash1)] * f64(sign)[0, :1]
    g1 = y[:, unstriped(hash2)] * f64(sign)[1, :1]
    g2 = y[:, unstriped(hash3)] * f64(sign)[2, :1]
    med = np.maximum(np.minimum(g0, g1), np.minimum(np.maximum(g0, g1), g2))
    return med * (sigmoid(3.0 * (np.abs(med) - (np.abs(g0 + g1 + g2 - (3.0 * med))) + f64(thr))))

@@ -1,0 +1,148 @@
+from contextlib import ExitStack
+
+import concourse.mybir as mybir
+from concourse.masks import make_identity
+
+F32 = mybir.dt.float32
+BF16 = mybir.dt.bfloat16
+I32 = mybir.dt.int32
+U32 = mybir.dt.uint32
+U16 = mybir.dt.uint16
+U8 = mybir.dt.uint8
+FP8X4 = mybir.dt.float8_e4m3fn_x4
+ALU = mybir.AluOpType
+ACT = mybir.ActivationFunctionType
+
+P = 128
+K, T, S, M, R = 1024, 2048, 512, 128, 512
+PASSES = 2
+FLOPS = 2 * K * M * S
+
+CH = 256
+
+
+def tile_picked_ycsk_heavy_p_kernel(tc, x_words, x_scales, w1, sign, thr, offs, hash1, hash2, hash3, out):
+    nc = tc.nc
+    with ExitStack() as ctx:
+        keep = ctx.enter_context(tc.tile_pool(name="keep", bufs=1))
+        psum = ctx.enter_context(tc.psum_pool(name="psum", bufs=1))
+
+        offs_sb = keep.tile([P, S // 16], U16, name="offs_sb")
+        nc.sync.dma_start(offs_sb[:], offs)
+
+        scale_table = keep.tile([P, T], U8, name="scale_table", align_bytes=64, tag="scales_then_words")
+        nc.gpsimd.memset(scale_table[:].bitcast(I32), 0)
+
+        w_raw = keep.tile([P, PASSES, 4, M], F32, name="w_raw", tag="w_then_sign")
+        nc.sync.dma_start(w_raw[:].rearrange("p o j m -> p o (j m)"), w1.rearrange("(o p j) m -> p o (j m)", o=PASSES, j=4))
+        word_table = []
+        for o in range(PASSES):
+            t = keep.tile([P, T], U32, name=f"word_table{o}", align_bytes=64)
+            nc.sync.dma_start(t[:].bitcast(I32), x_words[o].rearrange("p n t -> p (n t)").bitcast(I32))
+            word_table.append(t)
+        for q in range(4):
+            eng = nc.scalar if q < 2 else nc.gpsimd
+            eng.dma_start(scale_table[32 * q : 32 * q + 8, :].bitcast(I32), x_scales[:, 4 * q : 4 * q + 4, :].bitcast(I32))
+
+        warm = keep.tile([P, 1], F32, name="warm")
+        warm2 = keep.tile([P, 1], F32, name="warm2")
+        nc.vector.memset(warm[:], 0.0)
+        nc.scalar.activation(warm2[:], warm[:], ACT.Sigmoid)
+
+        hash_sb = []
+        for d, h in enumerate((hash1, hash2, hash3)):
+            t = keep.tile([P, R // 16], U16, name=f"hash_sb{d}")
+            nc.sync.dma_start(t[:], h)
+            hash_sb.append(t)
+
+        w_grouped = keep.tile([P, PASSES, M, 4], BF16, name="w_grouped", align_bytes=64)
+        nc.scalar.copy(w_grouped[:], w_raw[:].rearrange("p o j m -> p o m j"))
+        signs = keep.tile([P, 3 * R + 8], F32, name="signs", tag="w_then_sign")
+        sign_sb = [signs[:, d * R : (d + 1) * R] for d in range(3)]
+        for d in range(3):
+            nc.sync.dma_start(sign_sb[d], sign[d])
+        thr_sb = signs[:, 3 * R : 3 * R + 1]
+        nc.sync.dma_start(thr_sb, thr)
+        w_codes = keep.tile([P, PASSES * M], U32, name="w_codes", align_bytes=64)
+        w_scales = keep.tile([P, PASSES * M], U8, name="w_scales", align_bytes=64)
+        nc.vector.quantize_mx(out=w_codes[:].bitcast(FP8X4), scales=w_scales[:], in_=w_grouped[:].rearrange("p o m j -> p (o m j)"))
+
+        picked_scales = keep.tile([P, S], U8, name="picked_scales", align_bytes=64)
+        words0 = keep.tile([P, S], U32, name="words0", align_bytes=64)
+        nc.vector.tensor_copy(words0[:], word_table[0][:].indirect(offs_sb[:]))
+        nc.vector.tensor_copy(picked_scales[:], scale_table[:].indirect(offs_sb[:]))
+        y = keep.tile([P, S], F32, name="y")
+        for c in range(2):
+            cols = slice(c * 256, (c + 1) * 256)
+            w1h = keep.tile([P, 256], U32, name=f"words1_{c}", align_bytes=64, tag=("scales_then_words" if c == 0 else "words1_1"))
+            nc.vector.tensor_copy(w1h[:], word_table[1][:].indirect(offs_sb[:, c * 16 : (c + 1) * 16]))
+            acc = psum.tile([P, 256], F32, name=f"acc{c}")
+            for o in range(PASSES):
+                rhs = words0[:, cols] if o == 0 else w1h[:]
+                nc.tensor.matmul_mx(
+                    out=acc[:],
+                    lhsT=w_codes[:, o * M : (o + 1) * M].bitcast(FP8X4),
+                    lhsT_scale=w_scales[:, o * M : (o + 1) * M],
+                    rhs=rhs.bitcast(FP8X4),
+                    rhs_scale=picked_scales[4 * o :, cols],
+                    start=(o == 0),
+                    stop=(o == PASSES - 1),
+                )
+            nc.scalar.copy(y[:, cols], acc[:])
+
+        ident = keep.tile([P, P], F32, name="ident")
+        make_identity(nc, ident[:])
+        WA, WC = 384, 128
+        tl = lambda name, w, tag=None: keep.tile([P, w], F32, name=name, tag=tag or name)[:]
+        V, SC = nc.vector, nc.scalar
+
+        def gather(dst, d, r0, w):
+            V.tensor_tensor(dst, y[:].indirect(hash_sb[d][:, r0 // 16 : (r0 + w) // 16]), sign_sb[d][:, r0 : r0 + w], ALU.mult)
+
+        a1, a0, a2 = tl("a1", WA), tl("a0", WA), tl("a2", WA)
+        gather(a1, 1, 0, WA)
+        n1 = tl("n1", WA, "n1_c0")
+        SC.mul(n1, a1, -3.0)
+        gather(a0, 0, 0, WA)
+        gather(a2, 2, 0, WA)
+        nhi, nlo, nt, m3 = tl("nhi", WA), tl("nlo", WA, "nlo_c1"), tl("nt", WA, "nt_c2"), tl("m3", WA)
+        V.scalar_tensor_tensor(nhi, a0, -3.0, n1, ALU.mult, ALU.min)
+        V.scalar_tensor_tensor(nlo, a0, -3.0, n1, ALU.mult, ALU.max)
+        V.scalar_tensor_tensor(nt, a2, -3.0, nhi, ALU.mult, ALU.max)
+        c0 = tl("c0", WC, "n1_c0")
+        gather(c0, 0, WA, WC)
+        V.tensor_tensor(m3, nlo, nt, ALU.min)
+        back = psum.tile([P, WA], F32, name="back")
+        BT = tl("BT", WA)
+        for b in range(WA // P):
+            blk = slice(b * P, (b + 1) * P)
+            th = psum.tile([P, P], F32, name=f"there{b}")
+            for i, term in enumerate((a1, a0, a2, m3)):
+                nc.tensor.matmul(th[:], term[:, blk], ident[:], start=(i == 0), stop=(i == 3), is_transpose=True)
+            SC.activation(BT[:, blk], th[:], ACT.Abs)
+            nc.tensor.transpose(back[:, blk], BT[:, blk], ident[:])
+        AA = tl("AA", WA)
+        SC.activation(AA, m3, ACT.Abs, scale=1.0 / 3.0)
+        c1, c2 = tl("c1", WC, "nlo_c1"), tl("c2", WC, "nt_c2")
+        gather(c1, 1, WA, WC)
+        gather(c2, 2, WA, WC)
+        hi, lo, s01, t, s, med, dd, AC, BC = (tl(k, WC) for k in ("hi", "lo", "s01", "t", "s", "med", "dd", "AC", "BC"))
+        V.tensor_tensor(hi, c0, c1, ALU.max)
+        V.tensor_tensor(s01, c0, c1, ALU.add)
+        V.tensor_tensor(lo, c0, c1, ALU.min)
+        V.tensor_tensor(t, hi, c2, ALU.min)
+        V.tensor_tensor(s, s01, c2, ALU.add)
+        V.tensor_tensor(med, lo, t, ALU.max)
+        SC.activation(AC, med, ACT.Abs)
+        diffA, sigA, resA = tl("diffA", WA), tl("sigA", WA), tl("resA", WA)
+        diffC, sigC, resC = tl("diffC", WC), tl("sigC", WC), tl("resC", WC)
+        V.scalar_tensor_tensor(diffA, AA, thr_sb, back[:], ALU.add, ALU.subtract)
+        V.scalar_tensor_tensor(dd, med, -3.0, s, ALU.mult, ALU.add)
+        SC.activation(BC, dd, ACT.Abs)
+        SC.activation(sigA, diffA, ACT.Sigmoid, scale=3.0)
+        V.scalar_tensor_tensor(diffC, AC, thr_sb, BC, ALU.add, ALU.subtract)
+        V.scalar_tensor_tensor(resA, m3, -1.0 / 3.0, sigA, ALU.mult, ALU.mult)
+        nc.sync.dma_start(out[:, 0:WA], resA)
+        SC.activation(sigC, diffC, ACT.Sigmoid, scale=3.0)
+        V.tensor_tensor(resC, med, sigC, ALU.mult)
+        nc.sync.dma_start(out[:, WA:R], resC)

@@ -28,22 +28,24 @@ def tile_picked_ycsk_heavy_p_kernel(tc, x_words, x_scales, w1, sign, thr, offs, 
         psum = ctx.enter_context(tc.psum_pool(name="psum", bufs=1))
 
         offs_sb = keep.tile([P, S // 16], U16, name="offs_sb")
-        nc.sync.dma_start(offs_sb[:], offs)
 
         scale_table = keep.tile([P, T], U8, name="scale_table", align_bytes=64, tag="scales_then_words")
+        scale_rows = keep.tile([P, T // 4], I32, name="scale_rows", align_bytes=64)
         nc.gpsimd.memset(scale_table[:].bitcast(I32), 0)
 
         w_raw = keep.tile([P, PASSES, 4, M], F32, name="w_raw", tag="w_then_sign")
         nc.sync.dma_start(w_raw[:].rearrange("p o j m -> p o (j m)"), w1.rearrange("(o p j) m -> p o (j m)", o=PASSES, j=4))
+        nc.sync.dma_start(offs_sb[:], offs)
+        for q in range(4):
+            nc.sync.dma_start(scale_rows[32 * q : 32 * q + 8, :], x_scales[:, 4 * q : 4 * q + 4, :].bitcast(I32))
         word_table = []
         for o in range(PASSES):
             t = keep.tile([P, T], U32, name=f"word_table{o}", align_bytes=64)
             nc.sync.dma_start(t[:].bitcast(I32), x_words[o].rearrange("p n t -> p (n t)").bitcast(I32))
             word_table.append(t)
-        for q in range(4):
-            eng = nc.scalar if q < 2 else nc.gpsimd
-            eng.dma_start(scale_table[32 * q : 32 * q + 8, :].bitcast(I32), x_scales[:, 4 * q : 4 * q + 4, :].bitcast(I32))
 
+        for q in range(4):
+            nc.vector.tensor_copy(scale_table[32 * q : 32 * q + 8, :].bitcast(I32), scale_rows[32 * q : 32 * q + 8, :])
         warm = keep.tile([P, 1], F32, name="warm")
         warm2 = keep.tile([P, 1], F32, name="warm2")
         nc.vector.memset(warm[:], 0.0)
@@ -76,19 +78,24 @@ def tile_picked_ycsk_heavy_p_kernel(tc, x_words, x_scales, w1, sign, thr, offs, 
             cols = slice(c * 256, (c + 1) * 256)
             w1h = keep.tile([P, 256], U32, name=f"words1_{c}", align_bytes=64, tag=("scales_then_words" if c == 0 else "words1_1"))
             nc.vector.tensor_copy(w1h[:], word_table[1][:].indirect(offs_sb[:, c * 16 : (c + 1) * 16]))
-            acc = psum.tile([P, 256], F32, name=f"acc{c}")
-            for o in range(PASSES):
-                rhs = words0[:, cols] if o == 0 else w1h[:]
-                nc.tensor.matmul_mx(
-                    out=acc[:],
-                    lhsT=w_codes[:, o * M : (o + 1) * M].bitcast(FP8X4),
-                    lhsT_scale=w_scales[:, o * M : (o + 1) * M],
-                    rhs=rhs.bitcast(FP8X4),
-                    rhs_scale=picked_scales[4 * o :, cols],
-                    start=(o == 0),
-                    stop=(o == PASSES - 1),
-                )
-            nc.scalar.copy(y[:, cols], acc[:])
+            for part, (n0, n1) in enumerate(((0, 256),) if c == 0 else ((0, 128), (128, 256))):
+                acc = psum.tile([P, n1 - n0], F32, name=f"acc{c}_{part}")
+                ycols = slice(c * 256 + n0, c * 256 + n1)
+                for o in range(PASSES):
+                    rhs = words0[:, ycols] if o == 0 else w1h[:, n0:n1]
+                    nc.tensor.matmul_mx(
+                        out=acc[:],
+                        lhsT=w_codes[:, o * M : (o + 1) * M].bitcast(FP8X4),
+                        lhsT_scale=w_scales[:, o * M : (o + 1) * M],
+                        rhs=rhs.bitcast(FP8X4),
+                        rhs_scale=picked_scales[4 * o :, ycols],
+                        start=(o == 0),
+                        stop=(o == PASSES - 1),
+                    )
+                if part == 0:
+                    nc.scalar.copy(y[:, ycols], acc[:])
+                else:
+                    nc.vector.tensor_copy(y[:, ycols], acc[:])
 
         ident = keep.tile([P, P], F32, name="ident")
         make_identity(nc, ident[:])

@@ -33,14 +33,16 @@ def tile_picked_ycsk_heavy_p_kernel(tc, x_words, x_scales, w1, sign, thr, offs, 
         scale_rows = keep.tile([P, T // 4], I32, name="scale_rows", align_bytes=64)
         nc.gpsimd.memset(scale_table[:].bitcast(I32), 0)
 
+        for q in range(0, 2):
+            nc.sync.dma_start(scale_rows[32 * q : 32 * q + 8, :], x_scales[:, 4 * q : 4 * q + 4, :].bitcast(I32))
         w_raw = keep.tile([P, PASSES, 4, M], F32, name="w_raw", tag="w_then_sign")
         nc.sync.dma_start(w_raw[:].rearrange("p o j m -> p o (j m)"), w1.rearrange("(o p j) m -> p o (j m)", o=PASSES, j=4))
-        nc.sync.dma_start(offs_sb[:], offs)
-        for q in range(4):
+        for q in range(2, 4):
             nc.sync.dma_start(scale_rows[32 * q : 32 * q + 8, :], x_scales[:, 4 * q : 4 * q + 4, :].bitcast(I32))
+        nc.sync.dma_start(offs_sb[:], offs)
         word_table = []
         for o in range(PASSES):
-            t = keep.tile([P, T], U32, name=f"word_table{o}", align_bytes=64)
+            t = keep.tile([P, T], U32, name=f"word_table{o}", align_bytes=64, tag=f"table{o}")
             nc.sync.dma_start(t[:].bitcast(I32), x_words[o].rearrange("p n t -> p (n t)").bitcast(I32))
             word_table.append(t)
 
@@ -57,7 +59,9 @@ def tile_picked_ycsk_heavy_p_kernel(tc, x_words, x_scales, w1, sign, thr, offs, 
             nc.sync.dma_start(t[:], h)
             hash_sb.append(t)
 
-        w_grouped = keep.tile([P, PASSES, M, 4], BF16, name="w_grouped", align_bytes=64)
+        picked_scales = keep.tile([P, S], U8, name="picked_scales", align_bytes=64)
+        nc.vector.tensor_copy(picked_scales[:], scale_table[:].indirect(offs_sb[:]))
+        w_grouped = keep.tile([P, PASSES, M, 4], BF16, name="w_grouped", align_bytes=64, tag="grouped_then_words")
         nc.scalar.copy(w_grouped[:], w_raw[:].rearrange("p o j m -> p o m j"))
         signs = keep.tile([P, 3 * R + 8], F32, name="signs", tag="w_then_sign")
         sign_sb = [signs[:, d * R : (d + 1) * R] for d in range(3)]
@@ -69,14 +73,12 @@ def tile_picked_ycsk_heavy_p_kernel(tc, x_words, x_scales, w1, sign, thr, offs, 
         w_scales = keep.tile([P, PASSES * M], U8, name="w_scales", align_bytes=64)
         nc.vector.quantize_mx(out=w_codes[:].bitcast(FP8X4), scales=w_scales[:], in_=w_grouped[:].rearrange("p o m j -> p (o m j)"))
 
-        picked_scales = keep.tile([P, S], U8, name="picked_scales", align_bytes=64)
-        words0 = keep.tile([P, S], U32, name="words0", align_bytes=64)
+        words0 = keep.tile([P, S], U32, name="words0", align_bytes=64, tag="grouped_then_words")
         nc.vector.tensor_copy(words0[:], word_table[0][:].indirect(offs_sb[:]))
-        nc.vector.tensor_copy(picked_scales[:], scale_table[:].indirect(offs_sb[:]))
         y = keep.tile([P, S], F32, name="y")
         for c in range(2):
             cols = slice(c * 256, (c + 1) * 256)
-            w1h = keep.tile([P, 256], U32, name=f"words1_{c}", align_bytes=64, tag=("scales_then_words" if c == 0 else "words1_1"))
+            w1h = keep.tile([P, 256], U32, name=f"words1_{c}", align_bytes=64, tag=("table0" if c == 0 else "scales_then_words"))
             nc.vector.tensor_copy(w1h[:], word_table[1][:].indirect(offs_sb[:, c * 16 : (c + 1) * 16]))
             for part, (n0, n1) in enumerate(((0, 256),) if c == 0 else ((0, 128), (128, 256))):
                 acc = psum.tile([P, n1 - n0], F32, name=f"acc{c}_{part}")
@@ -102,25 +104,27 @@ def tile_picked_ycsk_heavy_p_kernel(tc, x_words, x_scales, w1, sign, thr, offs, 
         WA, WC = 384, 128
         tl = lambda name, w, tag=None: keep.tile([P, w], F32, name=name, tag=tag or name)[:]
         V, SC = nc.vector, nc.scalar
+        thr3 = tl("thr3", 1)
+        SC.mul(thr3, thr_sb, 3.0)
 
         def gather(dst, d, r0, w):
             V.tensor_tensor(dst, y[:].indirect(hash_sb[d][:, r0 // 16 : (r0 + w) // 16]), sign_sb[d][:, r0 : r0 + w], ALU.mult)
 
         a1, a0, a2 = tl("a1", WA), tl("a0", WA), tl("a2", WA)
         gather(a1, 1, 0, WA)
-        n1 = tl("n1", WA, "n1_c0")
+        n1 = tl("n1", WA, "n1_c1")
         SC.mul(n1, a1, -3.0)
         gather(a0, 0, 0, WA)
         gather(a2, 2, 0, WA)
-        nhi, nlo, nt, m3 = tl("nhi", WA), tl("nlo", WA, "nlo_c1"), tl("nt", WA, "nt_c2"), tl("m3", WA)
+        nhi, nlo, nt, m3 = tl("nhi", WA), tl("nlo", WA, "nlo_c0"), tl("nt", WA, "nt_c2"), tl("m3", WA)
         V.scalar_tensor_tensor(nhi, a0, -3.0, n1, ALU.mult, ALU.min)
         V.scalar_tensor_tensor(nlo, a0, -3.0, n1, ALU.mult, ALU.max)
         V.scalar_tensor_tensor(nt, a2, -3.0, nhi, ALU.mult, ALU.max)
-        c0 = tl("c0", WC, "n1_c0")
-        gather(c0, 0, WA, WC)
+        c1 = tl("c1", WC, "n1_c1")
+        gather(c1, 1, WA, WC)
         V.tensor_tensor(m3, nlo, nt, ALU.min)
-        back = psum.tile([P, WA], F32, name="back")
-        BT = tl("BT", WA)
+        back = psum.tile([P, WA], F32, name="back", tag="acc0_0")
+        BT, AA = tl("BT", WA), tl("AA", WA)
         for b in range(WA // P):
             blk = slice(b * P, (b + 1) * P)
             th = psum.tile([P, P], F32, name=f"there{b}")
@@ -128,28 +132,41 @@ def tile_picked_ycsk_heavy_p_kernel(tc, x_words, x_scales, w1, sign, thr, offs, 
                 nc.tensor.matmul(th[:], term[:, blk], ident[:], start=(i == 0), stop=(i == 3), is_transpose=True)
             SC.activation(BT[:, blk], th[:], ACT.Abs)
             nc.tensor.transpose(back[:, blk], BT[:, blk], ident[:])
-        AA = tl("AA", WA)
         SC.activation(AA, m3, ACT.Abs, scale=1.0 / 3.0)
-        c1, c2 = tl("c1", WC, "nlo_c1"), tl("c2", WC, "nt_c2")
-        gather(c1, 1, WA, WC)
+        c0, c2 = tl("c0", WC, "nlo_c0"), tl("c2", WC, "nt_c2")
+        gather(c0, 0, WA, WC)
         gather(c2, 2, WA, WC)
-        hi, lo, s01, t, s, med, dd, AC, BC = (tl(k, WC) for k in ("hi", "lo", "s01", "t", "s", "med", "dd", "AC", "BC"))
+        hi, lo, s01, t, s, med, dd, AC, nB, diffC, sigC, resC = (tl(k, WC) for k in ("hi", "lo", "s01", "t", "s", "med", "dd", "AC", "nB", "diffC", "sigC", "resC"))
         V.tensor_tensor(hi, c0, c1, ALU.max)
         V.tensor_tensor(s01, c0, c1, ALU.add)
-        V.tensor_tensor(lo, c0, c1, ALU.min)
         V.tensor_tensor(t, hi, c2, ALU.min)
+        V.tensor_tensor(lo, c0, c1, ALU.min)
         V.tensor_tensor(s, s01, c2, ALU.add)
         V.tensor_tensor(med, lo, t, ALU.max)
         SC.activation(AC, med, ACT.Abs)
-        diffA, sigA, resA = tl("diffA", WA), tl("sigA", WA), tl("resA", WA)
-        diffC, sigC, resC = tl("diffC", WC), tl("sigC", WC), tl("resC", WC)
-        V.scalar_tensor_tensor(diffA, AA, thr_sb, back[:], ALU.add, ALU.subtract)
+        halves = ((0, 192), (192, 384))
+        dA = [tl(f"diffA{j}", h1 - h0) for j, (h0, h1) in enumerate(halves)]
+        sA = [tl(f"sigA{j}", h1 - h0) for j, (h0, h1) in enumerate(halves)]
+        rA = [tl(f"resA{j}", h1 - h0) for j, (h0, h1) in enumerate(halves)]
+
+        def diff_a(j):
+            h0, h1 = halves[j]
+            V.tensor_tensor(dA[j], AA[:, h0:h1], back[:, h0:h1], ALU.subtract)
+            SC.activation(sA[j], dA[j], ACT.Sigmoid, scale=3.0, bias=thr3)
+
+        def res_a(j):
+            h0, h1 = halves[j]
+            V.scalar_tensor_tensor(rA[j], m3[:, h0:h1], -1.0 / 3.0, sA[j], ALU.mult, ALU.mult)
+            nc.sync.dma_start(out[:, h0:h1], rA[j])
+
+        diff_a(0)
         V.scalar_tensor_tensor(dd, med, -3.0, s, ALU.mult, ALU.add)
-        SC.activation(BC, dd, ACT.Abs)
-        SC.activation(sigA, diffA, ACT.Sigmoid, scale=3.0)
-        V.scalar_tensor_tensor(diffC, AC, thr_sb, BC, ALU.add, ALU.subtract)
-        V.scalar_tensor_tensor(resA, m3, -1.0 / 3.0, sigA, ALU.mult, ALU.mult)
-        nc.sync.dma_start(out[:, 0:WA], resA)
-        SC.activation(sigC, diffC, ACT.Sigmoid, scale=3.0)
+        for j in range(1, len(halves)):
+            diff_a(j)
+        V.scalar_tensor_tensor(nB, dd, -1.0, dd, ALU.mult, ALU.min)
+        V.tensor_tensor(diffC, AC, nB, ALU.add)
+        SC.activation(sigC, diffC, ACT.Sigmoid, scale=3.0, bias=thr3)
+        for j in range(len(halves)):
+            res_a(j)
         V.tensor_tensor(resC, med, sigC, ALU.mult)
         nc.sync.dma_start(out[:, WA:R], resC)

from contextlib import ExitStack

import concourse.mybir as mybir
from concourse.masks import make_identity

F32 = mybir.dt.float32
BF16 = mybir.dt.bfloat16
I32 = mybir.dt.int32
U32 = mybir.dt.uint32
U16 = mybir.dt.uint16
U8 = mybir.dt.uint8
FP8X4 = mybir.dt.float8_e4m3fn_x4
ALU = mybir.AluOpType
ACT = mybir.ActivationFunctionType

P = 128
K, T, S, M, R = 1024, 2048, 512, 128, 512
PASSES = 2
FLOPS = 2 * K * M * S

CH = 256


def tile_picked_ycsk_heavy_p_kernel(tc, x_words, x_scales, w1, sign, thr, offs, hash1, hash2, hash3, out):
    nc = tc.nc
    with ExitStack() as ctx:
        keep = ctx.enter_context(tc.tile_pool(name="keep", bufs=1))
        psum = ctx.enter_context(tc.psum_pool(name="psum", bufs=1))

        offs_sb = keep.tile([P, S // 16], U16, name="offs_sb")

        scale_table = keep.tile([P, T], U8, name="scale_table", align_bytes=64, tag="scales_then_words")
        scale_rows = keep.tile([P, T // 4], I32, name="scale_rows", align_bytes=64)
        nc.gpsimd.memset(scale_table[:].bitcast(I32), 0)

        for q in range(0, 2):
            nc.sync.dma_start(scale_rows[32 * q : 32 * q + 8, :], x_scales[:, 4 * q : 4 * q + 4, :].bitcast(I32))
        w_raw = keep.tile([P, PASSES, 4, M], F32, name="w_raw", tag="w_then_sign")
        nc.sync.dma_start(w_raw[:].rearrange("p o j m -> p o (j m)"), w1.rearrange("(o p j) m -> p o (j m)", o=PASSES, j=4))
        for q in range(2, 4):
            nc.sync.dma_start(scale_rows[32 * q : 32 * q + 8, :], x_scales[:, 4 * q : 4 * q + 4, :].bitcast(I32))
        nc.sync.dma_start(offs_sb[:], offs)
        word_table = []
        for o in range(PASSES):
            t = keep.tile([P, T], U32, name=f"word_table{o}", align_bytes=64, tag=f"table{o}")
            nc.sync.dma_start(t[:].bitcast(I32), x_words[o].rearrange("p n t -> p (n t)").bitcast(I32))
            word_table.append(t)

        for q in range(4):
            nc.vector.tensor_copy(scale_table[32 * q : 32 * q + 8, :].bitcast(I32), scale_rows[32 * q : 32 * q + 8, :])
        warm = keep.tile([P, 1], F32, name="warm")
        warm2 = keep.tile([P, 1], F32, name="warm2")
        nc.vector.memset(warm[:], 0.0)
        nc.scalar.activation(warm2[:], warm[:], ACT.Sigmoid)

        hash_sb = []
        for d, h in enumerate((hash1, hash2, hash3)):
            t = keep.tile([P, R // 16], U16, name=f"hash_sb{d}")
            nc.sync.dma_start(t[:], h)
            hash_sb.append(t)

        picked_scales = keep.tile([P, S], U8, name="picked_scales", align_bytes=64)
        nc.vector.tensor_copy(picked_scales[:], scale_table[:].indirect(offs_sb[:]))
        w_grouped = keep.tile([P, PASSES, M, 4], BF16, name="w_grouped", align_bytes=64, tag="grouped_then_words")
        nc.scalar.copy(w_grouped[:], w_raw[:].rearrange("p o j m -> p o m j"))
        signs = keep.tile([P, 3 * R + 8], F32, name="signs", tag="w_then_sign")
        sign_sb = [signs[:, d * R : (d + 1) * R] for d in range(3)]
        for d in range(3):
            nc.sync.dma_start(sign_sb[d], sign[d])
        thr_sb = signs[:, 3 * R : 3 * R + 1]
        nc.sync.dma_start(thr_sb, thr)
        w_codes = keep.tile([P, PASSES * M], U32, name="w_codes", align_bytes=64)
        w_scales = keep.tile([P, PASSES * M], U8, name="w_scales", align_bytes=64)
        nc.vector.quantize_mx(out=w_codes[:].bitcast(FP8X4), scales=w_scales[:], in_=w_grouped[:].rearrange("p o m j -> p (o m j)"))

        words0 = keep.tile([P, S], U32, name="words0", align_bytes=64, tag="grouped_then_words")
        nc.vector.tensor_copy(words0[:], word_table[0][:].indirect(offs_sb[:]))
        y = keep.tile([P, S], F32, name="y")
        for c in range(2):
            cols = slice(c * 256, (c + 1) * 256)
            w1h = keep.tile([P, 256], U32, name=f"words1_{c}", align_bytes=64, tag=("table0" if c == 0 else "scales_then_words"))
            nc.vector.tensor_copy(w1h[:], word_table[1][:].indirect(offs_sb[:, c * 16 : (c + 1) * 16]))
            for part, (n0, n1) in enumerate(((0, 256),) if c == 0 else ((0, 128), (128, 256))):
                acc = psum.tile([P, n1 - n0], F32, name=f"acc{c}_{part}")
                ycols = slice(c * 256 + n0, c * 256 + n1)
                for o in range(PASSES):
                    rhs = words0[:, ycols] if o == 0 else w1h[:, n0:n1]
                    nc.tensor.matmul_mx(
                        out=acc[:],
                        lhsT=w_codes[:, o * M : (o + 1) * M].bitcast(FP8X4),
                        lhsT_scale=w_scales[:, o * M : (o + 1) * M],
                        rhs=rhs.bitcast(FP8X4),
                        rhs_scale=picked_scales[4 * o :, ycols],
                        start=(o == 0),
                        stop=(o == PASSES - 1),
                    )
                if part == 0:
                    nc.scalar.copy(y[:, ycols], acc[:])
                else:
                    nc.vector.tensor_copy(y[:, ycols], acc[:])

        ident = keep.tile([P, P], F32, name="ident")
        make_identity(nc, ident[:])
        WA, WC = 384, 128
        tl = lambda name, w, tag=None: keep.tile([P, w], F32, name=name, tag=tag or name)[:]
        V, SC = nc.vector, nc.scalar
        thr3 = tl("thr3", 1)
        SC.mul(thr3, thr_sb, 3.0)

        def gather(dst, d, r0, w):
            V.tensor_tensor(dst, y[:].indirect(hash_sb[d][:, r0 // 16 : (r0 + w) // 16]), sign_sb[d][:, r0 : r0 + w], ALU.mult)

        a1, a0, a2 = tl("a1", WA), tl("a0", WA), tl("a2", WA)
        gather(a1, 1, 0, WA)
        n1 = tl("n1", WA, "n1_c1")
        SC.mul(n1, a1, -3.0)
        gather(a0, 0, 0, WA)
        gather(a2, 2, 0, WA)
        nhi, nlo, nt, m3 = tl("nhi", WA), tl("nlo", WA, "nlo_c0"), tl("nt", WA, "nt_c2"), tl("m3", WA)
        V.scalar_tensor_tensor(nhi, a0, -3.0, n1, ALU.mult, ALU.min)
        V.scalar_tensor_tensor(nlo, a0, -3.0, n1, ALU.mult, ALU.max)
        V.scalar_tensor_tensor(nt, a2, -3.0, nhi, ALU.mult, ALU.max)
        c1 = tl("c1", WC, "n1_c1")
        gather(c1, 1, WA, WC)
        V.tensor_tensor(m3, nlo, nt, ALU.min)
        back = psum.tile([P, WA], F32, name="back", tag="acc0_0")
        BT, AA = tl("BT", WA), tl("AA", WA)
        for b in range(WA // P):
            blk = slice(b * P, (b + 1) * P)
            th = psum.tile([P, P], F32, name=f"there{b}")
            for i, term in enumerate((a1, a0, a2, m3)):
                nc.tensor.matmul(th[:], term[:, blk], ident[:], start=(i == 0), stop=(i == 3), is_transpose=True)
            SC.activation(BT[:, blk], th[:], ACT.Abs)
            nc.tensor.transpose(back[:, blk], BT[:, blk], ident[:])
        SC.activation(AA, m3, ACT.Abs, scale=1.0 / 3.0)
        c0, c2 = tl("c0", WC, "nlo_c0"), tl("c2", WC, "nt_c2")
        gather(c0, 0, WA, WC)
        gather(c2, 2, WA, WC)
        hi, lo, s01, t, s, med, dd, AC, nB, diffC, sigC, resC = (tl(k, WC) for k in ("hi", "lo", "s01", "t", "s", "med", "dd", "AC", "nB", "diffC", "sigC", "resC"))
        V.tensor_tensor(hi, c0, c1, ALU.max)
        V.tensor_tensor(s01, c0, c1, ALU.add)
        V.tensor_tensor(t, hi, c2, ALU.min)
        V.tensor_tensor(lo, c0, c1, ALU.min)
        V.tensor_tensor(s, s01, c2, ALU.add)
        V.tensor_tensor(med, lo, t, ALU.max)
        SC.activation(AC, med, ACT.Abs)
        halves = ((0, 192), (192, 384))
        dA = [tl(f"diffA{j}", h1 - h0) for j, (h0, h1) in enumerate(halves)]
        sA = [tl(f"sigA{j}", h1 - h0) for j, (h0, h1) in enumerate(halves)]
        rA = [tl(f"resA{j}", h1 - h0) for j, (h0, h1) in enumerate(halves)]

        def diff_a(j):
            h0, h1 = halves[j]
            V.tensor_tensor(dA[j], AA[:, h0:h1], back[:, h0:h1], ALU.subtract)
            SC.activation(sA[j], dA[j], ACT.Sigmoid, scale=3.0, bias=thr3)

        def res_a(j):
            h0, h1 = halves[j]
            V.scalar_tensor_tensor(rA[j], m3[:, h0:h1], -1.0 / 3.0, sA[j], ALU.mult, ALU.mult)
            nc.sync.dma_start(out[:, h0:h1], rA[j])

        diff_a(0)
        V.scalar_tensor_tensor(dd, med, -3.0, s, ALU.mult, ALU.add)
        for j in range(1, len(halves)):
            diff_a(j)
        V.scalar_tensor_tensor(nB, dd, -1.0, dd, ALU.mult, ALU.min)
        V.tensor_tensor(diffC, AC, nB, ALU.add)
        SC.activation(sigC, diffC, ACT.Sigmoid, scale=3.0, bias=thr3)
        for j in range(len(halves)):
            res_a(j)
        V.tensor_tensor(resC, med, sigC, ALU.mult)
        nc.sync.dma_start(out[:, WA:R], resC)
